import numpy as np
import ml_dtypes


def mxq(x, axis, fmt="e4m3"):
    dtype, down = {"e4m3": (ml_dtypes.float8_e4m3fn, 7), "e5m2": (ml_dtypes.float8_e5m2, 14)}[fmt]
    v = np.moveaxis(np.asarray(x, np.float32).astype(ml_dtypes.bfloat16).astype(np.float64), axis, -1)
    blocks = v.reshape(v.shape[:-1] + (-1, 32))
    amax = np.abs(blocks).max(-1, keepdims=True)
    byte = np.maximum(np.where(amax > 0, np.frexp(amax)[1] - 1 + 127, 0) - down, 1)
    scale = np.exp2(byte - 127.0)
    codes = (blocks / scale).astype(np.float32).astype(dtype).astype(np.float64)
    return np.moveaxis((codes * scale).reshape(v.shape), -1, axis)


WIDE = False


def mx_kscale(k):
    if not WIDE:
        return np.ones(k)
    levels = np.array([10, -10, 5, -5, 0])
    if k % 512:
        return np.exp2(np.random.permutation(np.resize(levels, k // 32))).repeat(32)
    a = np.empty((k // 512, 16))
    for p in range(k // 512):
        a[p, :8] = np.random.permutation(np.resize(levels, 8))
        for g in range(8):
            far = levels[np.abs(levels - a[p, g]) >= 10]
            a[p, g + 8] = far[np.random.randint(len(far))]
    return np.exp2(a.ravel()).repeat(32)


def f64(x):
    return np.asarray(x).astype(np.float64)


def striped(idx):
    return np.tile(np.asarray(idx).reshape(-1, 16).T, (8, 1)).astype(np.uint16)


def unstriped(offs):
    return offs[:16].T.reshape(-1).astype(np.int64)


E2M1 = np.array([0.0, 0.5, 1.0, 1.5, 2.0, 3.0, 4.0, 6.0, -0.0, -0.5, -1.0, -1.5, -2.0, -3.0, -4.0, -6.0])


def pack_weight(w, fmt):
    k, n = w.shape
    w = f64(np.asarray(w, np.float32).astype(ml_dtypes.bfloat16)).reshape(k // 32, 32, n)
    amax = np.abs(w).max(1)
    if fmt == "e4m3":
        byte = np.frexp(amax)[1] - 1 + 127 - 7
    else:
        mant, ex = np.frexp(amax / 6.0)
        byte = np.where(mant > 0.5, ex, ex - 1) + 127
    byte = np.clip(np.where(amax > 0, byte, 1), 1, 254)
    scaled = (w * np.exp2(127.0 - byte)[:, None, :]).reshape(k, n).astype(np.float32)
    by_word = np.ascontiguousarray(scaled.reshape(k // 512, 128, 4, n).transpose(0, 1, 3, 2))
    if fmt == "e4m3":
        words = by_word.astype(ml_dtypes.float8_e4m3fn).view(np.uint8)
    else:
        c = by_word.astype(ml_dtypes.float4_e2m1fn).view(np.uint8) & 0xF
        words = (c[..., 0::2] | (c[..., 1::2] << 4)).reshape(k // 512, 128, 2 * n)
    return np.ascontiguousarray(words), np.ascontiguousarray(byte.astype(np.uint8).reshape(k // 512, 16, n))


def unpack_weight(words, scales, fmt):
    g, _, n = scales.shape
    words = np.ascontiguousarray(words).reshape(g, 128, n, -1)
    if fmt == "e4m3":
        vals = words.view(ml_dtypes.float8_e4m3fn).astype(np.float64)
    else:
        nib = np.empty((g, 128, n, 4), np.uint8)
        nib[..., 0::2] = words & 0xF
        nib[..., 1::2] = words >> 4
        vals = E2M1[nib]
    vals = vals * np.repeat(np.exp2(scales.astype(np.float64) - 127.0), 8, axis=1)[..., None]
    return vals.transpose(0, 1, 3, 2).reshape(g * 512, n)


def sigmoid(v):
    return 1.0 / (1.0 + np.exp(-v))


D, E, T, I, Q = 512, 512, 2048, 512, 128


def setup_inputs():
    n = np.random.standard_normal
    idx = np.random.permutation(T)[:I]
    fd = mx_kscale(D)
    fe = mx_kscale(E)
    keysp = pack_weight(n((D, T)) / fd[:, None], "e2m1")
    valsp = pack_weight(n((E, T)) / fe[:, None], "e2m1")
    return {
        "query": (n((D, Q)) * 0.8 / np.sqrt(D) * fd[:, None]).astype(np.float32),
        "keys_words": keysp[0],
        "keys_scales": keysp[1],
        "share": (np.random.uniform(0.2, 0.8, (Q, 1))).astype(np.float32),
        "gout": (n((E, Q)) * 1 / np.sqrt(E) * fe[:, None]).astype(np.float32),
        "vals_words": valsp[0],
        "vals_scales": valsp[1],
        "dquery": (n((D, Q)) * 1.0 / np.sqrt(D) * fd[:, None]).astype(np.float32),
        "base": (0.5 * n((Q, T))).astype(np.float32),
        "offs": striped(idx),
    }


def reference(query, keys_words, keys_scales, share, gout, vals_words, vals_scales, dquery, base, offs):
    idx = unstriped(offs)
    keysu = unpack_weight(keys_words, keys_scales, "e2m1")
    valsu = unpack_weight(vals_words, vals_scales, "e2m1")
    queryq = mxq(f64(query), 0, "e4m3")
    keysidxg = keysu[:, idx]
    a = queryq.T @ keysidxg
    dqueryq = mxq(f64(dquery), 0, "e4m3")
    ta = dqueryq.T @ keysidxg
    e0 = np.exp(a)
    s0 = sigmoid(a)
    p = e0 * f64(share) + s0 * (1.0 - f64(share)) * 3.0
    z = np.sum(p, axis=1, keepdims=True)
    goutq = mxq(f64(gout), 0, "e4m3")
    valsidxg = valsu[:, idx]
    c0 = goutq.T @ valsidxg
    dz = np.sum(c0 * p / np.square(z) * (-1.0), axis=1, keepdims=True)
    dp = c0 / z + dz
    ds0 = dp * 3.0 * (1.0 - f64(share))
    de0 = dp * f64(share)
    te0 = ta * e0
    ts0 = ta * s0 * (1.0 - s0)
    tp = te0 * f64(share) + ts0 * (1.0 - f64(share)) * 3.0
    tz = np.sum(tp, axis=1, keepdims=True)
    tdz = np.sum((tp * c0 - tz * z * 2.0 * c0 * p / np.square(z)) / np.square(z) * (-1.0), axis=1, keepdims=True)
    tdp = tz * c0 / np.square(z) * (-1.0) + tdz
    tds0 = tdp * 3.0 * (1.0 - f64(share))
    tde0 = tdp * f64(share)
    tda = (tds0 * s0 + ts0 * ds0) * (1.0 - s0) + ts0 * (-1.0) * ds0 * s0 + tde0 * e0 + te0 * de0
    gs = tda * 512.0
    gf = np.zeros((Q, T))
    gf[:, idx] = gs
    y = f64(base) + gf
    return y

@@ -1,0 +1,175 @@
+from contextlib import ExitStack
+
+import concourse.mybir as mybir
+
+D, T, I, Q = 512, 2048, 512, 128
+FLOPS = 3 * 2 * D * Q * I
+
+F32 = mybir.dt.float32
+BF16 = mybir.dt.bfloat16
+I32 = mybir.dt.int32
+U32 = mybir.dt.uint32
+U16 = mybir.dt.uint16
+U8 = mybir.dt.uint8
+FP8X4 = mybir.dt.float8_e4m3fn_x4
+FP4X4 = mybir.dt.float4_e2m1fn_x4
+ALU = mybir.AluOpType
+ACT = mybir.ActivationFunctionType
+
+P = 128
+PACK = 4
+BASE_PARTS = (768, 768, 512)
+STORE_PARTS = ((384, 384), (384, 384), (256, 256))
+
+
+def tile_attend_hvmixedparts_s_kernel(tc, query, keys_words, keys_scales, share, gout, vals_words, vals_scales, dquery, base, offs, out):
+    nc = tc.nc
+    with ExitStack() as ctx:
+        keep = ctx.enter_context(tc.tile_pool(name="keep", bufs=1))
+        stage = ctx.enter_context(tc.tile_pool(name="stage", bufs=3))
+        psum = ctx.enter_context(tc.psum_pool(name="psum", bufs=1))
+
+        def wide(name):
+            return keep.tile([P, I], F32, name=name)
+
+        def column(name):
+            return keep.tile([P, 1], F32, name=name)
+
+        offsets = keep.tile([P, I // 16], U16, name="offsets")
+        key_words = keep.tile([P, T], U16, name="key_words")
+        key_bytes = keep.tile([P, T], U8, name="key_bytes")
+        val_words = keep.tile([P, T], U16, name="val_words")
+        val_bytes = keep.tile([P, T], U8, name="val_bytes")
+        window = keep.tile([P, T], F32, name="window")
+
+        nc.vector.memset(key_bytes[:].bitcast(I32), 0)
+        nc.vector.memset(window[:], 0.0)
+        nc.vector.memset(val_bytes[:].bitcast(I32), 0)
+
+        def load_bytes(tile, src):
+            for quad in range(4):
+                nc.sync.dma_start(out=tile[32 * quad : 32 * quad + 4, :].bitcast(I32), in_=src[0, 4 * quad : 4 * quad + 4, :].bitcast(I32))
+
+        def load_rows(src, name):
+            raw = stage.tile([P, PACK, Q], F32, name=name, tag="stage")
+            nc.sync.dma_start(out=raw[:], in_=src.rearrange("(p j) w -> p j w", j=PACK))
+            return raw
+
+        s = column("s")
+        nc.gpsimd.dma_start(out=s[:], in_=share)
+        nc.sync.dma_start(offsets[:], offs)
+        nc.sync.dma_start(out=key_words[:].bitcast(I32), in_=keys_words[0].bitcast(I32))
+        load_bytes(key_bytes, keys_scales)
+        raw_q = load_rows(query, "raw_q")
+        raw_dq = load_rows(dquery, "raw_dq")
+        raw_g = load_rows(gout, "raw_g")
+        nc.sync.dma_start(out=val_words[:].bitcast(I32), in_=vals_words[0].bitcast(I32))
+        load_bytes(val_bytes, vals_scales)
+
+        r4, nr4, r2, r2i = column("r4"), column("nr4"), column("r2"), column("r2i")
+        nc.gpsimd.tensor_scalar(r4[:], s[:], -0.75, 0.75, ALU.mult, ALU.add)
+        nc.gpsimd.tensor_scalar(nr4[:], s[:], 0.75, -0.75, ALU.mult, ALU.add)
+        nc.gpsimd.tensor_scalar(r2[:], s[:], -1.5, 1.5, ALU.mult, ALU.add)
+        nc.gpsimd.tensor_scalar(r2i[:], s[:], -1.5 * I, 1.5 * I, ALU.mult, ALU.add)
+
+        def interleave(raw, name):
+            grouped = keep.tile([P, Q, PACK], BF16, name=name, align_bytes=64)
+            nc.scalar.activation(grouped[:], raw[:].rearrange("p j w -> p w j"), ACT.Copy)
+            return grouped
+
+        def quantize(grouped, name):
+            codes = keep.tile([P, Q], U32, name=name + "_codes", align_bytes=64)
+            scales = keep.tile([P, Q], U8, name=name + "_scales", align_bytes=64)
+            nc.vector.quantize_mx(out=codes[:].bitcast(FP8X4), scales=scales[:], in_=grouped[:].rearrange("p w j -> p (w j)"))
+            return codes, scales
+
+        def gather(tile, dtype, name):
+            picked = keep.tile([P, I], dtype, name=name, align_bytes=64)
+            nc.vector.tensor_copy(picked[:], tile[:].indirect(offsets[:]))
+            return picked
+
+        def product(rows, words, scale_bytes, name):
+            acc = psum.tile([P, I], F32, name=name)
+            nc.tensor.matmul_mx(out=acc[:], lhsT=rows[0][:].bitcast(FP8X4), lhsT_scale=rows[1][:], rhs=words[:].bitcast(FP4X4), rhs_scale=scale_bytes[:], start=True, stop=True)
+            return acc
+
+        grouped_q = interleave(raw_q, "grouped_q")
+        grouped_dq = interleave(raw_dq, "grouped_dq")
+        grouped_g = interleave(raw_g, "grouped_g")
+
+        base_parts = []
+        col = 0
+        for n, width in enumerate(BASE_PARTS):
+            part = stage.tile([P, width], F32, name="base%d" % n, tag="stage")
+            nc.sync.dma_start(out=part[:], in_=base[:, col : col + width])
+            base_parts.append(part)
+            col = col + width
+
+        picked_kb = gather(key_bytes, U8, "picked_kb")
+        picked_kw = gather(key_words, U16, "picked_kw")
+        mx_q = quantize(grouped_q, "q")
+        a = product(mx_q, picked_kw, picked_kb, "a")
+        mx_dq = quantize(grouped_dq, "dq")
+        ta = product(mx_dq, picked_kw, picked_kb, "ta")
+        picked_vw = gather(val_words, U16, "picked_vw")
+        mx_g = quantize(grouped_g, "g")
+        picked_vb = gather(val_bytes, U8, "picked_vb")
+        c = product(mx_g, picked_vw, picked_vb, "c")
+
+        e, th, th2, rs1 = wide("e"), wide("th"), wide("th2"), wide("rs1")
+        sum_e, sum_th = column("sum_e"), column("sum_th")
+        nc.scalar.activation(e[:], a[:], ACT.Exp, accum_out=sum_e[:])
+        nc.scalar.activation(th[:], a[:], ACT.Tanh, scale=0.5, accum_out=sum_th[:])
+        nc.scalar.activation(th2[:], th[:], ACT.Square)
+        nc.scalar.activation(rs1[:], th2[:], ACT.Identity, bias=r4[:], scale=nr4[:])
+
+        se_r4, se = wide("se_r4"), wide("se")
+        nc.gpsimd.tensor_scalar(se_r4[:], e[:], s[:], r4[:], ALU.mult, ALU.add)
+        nc.gpsimd.tensor_scalar(se[:], e[:], s[:], 0.0, ALU.mult, ALU.add)
+
+        z_sig, z, rz, nscale, nscale_rz = column("z_sig"), column("z"), column("rz"), column("nscale"), column("nscale_rz")
+        nc.scalar.activation(z_sig[:], sum_th[:], ACT.Identity, bias=r2i[:], scale=r2[:])
+        nc.scalar.activation(z[:], sum_e[:], ACT.Identity, bias=z_sig[:], scale=s[:])
+
+        p1 = wide("p1")
+        nc.vector.scalar_tensor_tensor(p1[:], th2[:], nr4[:], se_r4[:], ALU.mult, ALU.add)
+        nc.vector.reciprocal(rz[:], z[:])
+        nc.scalar.activation(nscale[:], rz[:], ACT.Copy, scale=-512.0)
+        nc.scalar.activation(nscale_rz[:], rz[:], ACT.Copy, scale=nscale[:])
+
+        trs1, p2 = wide("trs1"), wide("p2")
+        nc.gpsimd.tensor_tensor(trs1[:], th[:], rs1[:], ALU.mult)
+        nc.gpsimd.tensor_tensor(p2[:], se[:], trs1[:], ALU.subtract)
+
+        sum_ce, sum_ct, sum_cp, mean_c = column("sum_ce"), column("sum_ct"), column("sum_cp"), column("mean_c")
+        ce, ct = wide("ce"), wide("ct")
+        nc.vector.scalar_tensor_tensor(ce[:], c[:], s[:], e[:], ALU.mult, ALU.mult, accum_out=sum_ce[:])
+        nc.vector.scalar_tensor_tensor(ct[:], th[:], 1.0, c[:], ALU.add, ALU.mult, accum_out=sum_ct[:])
+        nc.scalar.activation(sum_cp[:], sum_ct[:], ACT.Identity, bias=sum_ce[:], scale=r2[:])
+        nc.scalar.activation(mean_c[:], sum_cp[:], ACT.Copy, scale=rz[:])
+
+        tp, tz = wide("tp"), column("tz")
+        nc.vector.scalar_tensor_tensor(tp[:], ta[:], 1.0, p1[:], ALU.mult, ALU.mult, accum_out=tz[:])
+        p1n = wide("p1n")
+        nc.scalar.activation(p1n[:], p1[:], ACT.Copy, scale=nscale_rz[:])
+
+        ctp, sum_ctp = wide("ctp"), column("sum_ctp")
+        nc.vector.scalar_tensor_tensor(ctp[:], c[:], mean_c[:], tp[:], ALU.subtract, ALU.mult, accum_out=sum_ctp[:])
+        row_term = wide("row_term")
+        nc.scalar.activation(row_term[:], p1n[:], ACT.Copy, scale=sum_ctp[:])
+
+        t2n, slope, slot_term = wide("t2n"), wide("slope"), wide("slot_term")
+        nc.vector.scalar_tensor_tensor(t2n[:], ta[:], nscale[:], p2[:], ALU.mult, ALU.mult)
+        nc.vector.scalar_tensor_tensor(slope[:], p1n[:], tz[:], t2n[:], ALU.mult, ALU.subtract)
+        nc.vector.scalar_tensor_tensor(slot_term[:], c[:], mean_c[:], slope[:], ALU.subtract, ALU.mult)
+        nc.vector.tensor_tensor(window[:].indirect(offsets[:]), slot_term[:], row_term[:], ALU.add)
+
+        col = 0
+        for n, widths in enumerate(STORE_PARTS):
+            inner = 0
+            for m, width in enumerate(widths):
+                result = keep.tile([P, width], F32, name="result%d_%d" % (n, m))
+                nc.vector.tensor_tensor(result[:], window[:, col : col + width], base_parts[n][:, inner : inner + width], ALU.add)
+                nc.sync.dma_start(out=out[:, col : col + width], in_=result[:])
+                col = col + width
+                inner = inner + width

@@ -18,15 +18,15 @@ ACT = mybir.ActivationFunctionType
 
 P = 128
 PACK = 4
-BASE_PARTS = (768, 768, 512)
-STORE_PARTS = ((384, 384), (384, 384), (256, 256))
+BASE_PARTS = (1024, 1024)
+STORE_PARTS = ((256, 384, 384), (512, 384, 128))
+HALF = I // 2
 
 
 def tile_attend_hvmixedparts_s_kernel(tc, query, keys_words, keys_scales, share, gout, vals_words, vals_scales, dquery, base, offs, out):
     nc = tc.nc
     with ExitStack() as ctx:
         keep = ctx.enter_context(tc.tile_pool(name="keep", bufs=1))
-        stage = ctx.enter_context(tc.tile_pool(name="stage", bufs=3))
         psum = ctx.enter_context(tc.psum_pool(name="psum", bufs=1))
 
         def wide(name):
@@ -36,35 +36,36 @@ def tile_attend_hvmixedparts_s_kernel(tc, query, keys_words, keys_scales, share,
             return keep.tile([P, 1], F32, name=name)
 
         offsets = keep.tile([P, I // 16], U16, name="offsets")
-        key_words = keep.tile([P, T], U16, name="key_words")
+        key_words = keep.tile([P, T], U16, name="key_words", tag="words_then_base")
         key_bytes = keep.tile([P, T], U8, name="key_bytes")
         val_words = keep.tile([P, T], U16, name="val_words")
-        val_bytes = keep.tile([P, T], U8, name="val_bytes")
+        val_bytes = keep.tile([P, T], U8, name="val_bytes", tag="bytes_then_p1")
         window = keep.tile([P, T], F32, name="window")
 
         nc.vector.memset(key_bytes[:].bitcast(I32), 0)
-        nc.vector.memset(window[:], 0.0)
         nc.vector.memset(val_bytes[:].bitcast(I32), 0)
+        nc.vector.memset(window[:], 0.0)
 
-        def load_bytes(tile, src):
-            for quad in range(4):
-                nc.sync.dma_start(out=tile[32 * quad : 32 * quad + 4, :].bitcast(I32), in_=src[0, 4 * quad : 4 * quad + 4, :].bitcast(I32))
+        def load_bytes(queue, tile, src, quads):
+            for quad in quads:
+                queue.dma_start(out=tile[32 * quad : 32 * quad + 4, :].bitcast(I32), in_=src[0, 4 * quad : 4 * quad + 4, :].bitcast(I32))
 
-        def load_rows(src, name):
-            raw = stage.tile([P, PACK, Q], F32, name=name, tag="stage")
-            nc.sync.dma_start(out=raw[:], in_=src.rearrange("(p j) w -> p j w", j=PACK))
+        def load_rows(queue, tag, src, name):
+            raw = keep.tile([P, PACK, Q], F32, name=name, tag=tag)
+            queue.dma_start(out=raw[:], in_=src.rearrange("(p j) w -> p j w", j=PACK))
             return raw
 
         s = column("s")
-        nc.gpsimd.dma_start(out=s[:], in_=share)
         nc.sync.dma_start(offsets[:], offs)
+        nc.scalar.dma_start(out=s[:], in_=share)
         nc.sync.dma_start(out=key_words[:].bitcast(I32), in_=keys_words[0].bitcast(I32))
-        load_bytes(key_bytes, keys_scales)
-        raw_q = load_rows(query, "raw_q")
-        raw_dq = load_rows(dquery, "raw_dq")
-        raw_g = load_rows(gout, "raw_g")
+        load_bytes(nc.sync, key_bytes, keys_scales, (0, 1))
+        load_bytes(nc.scalar, key_bytes, keys_scales, (2, 3))
+        raw_q = load_rows(nc.scalar, "q_then_base", query, "raw_q")
+        raw_dq = load_rows(nc.gpsimd, "dq_then_th", dquery, "raw_dq")
+        raw_g = load_rows(nc.sync, "g_then_e", gout, "raw_g")
         nc.sync.dma_start(out=val_words[:].bitcast(I32), in_=vals_words[0].bitcast(I32))
-        load_bytes(val_bytes, vals_scales)
+        load_bytes(nc.sync, val_bytes, vals_scales, range(4))
 
         r4, nr4, r2, r2i = column("r4"), column("nr4"), column("r2"), column("r2i")
         nc.gpsimd.tensor_scalar(r4[:], s[:], -0.75, 0.75, ALU.mult, ALU.add)
@@ -94,75 +95,94 @@ def tile_attend_hvmixedparts_s_kernel(tc, query, keys_words, keys_scales, share,
             return acc
 
         grouped_q = interleave(raw_q, "grouped_q")
-        grouped_dq = interleave(raw_dq, "grouped_dq")
         grouped_g = interleave(raw_g, "grouped_g")
-
-        base_parts = []
-        col = 0
-        for n, width in enumerate(BASE_PARTS):
-            part = stage.tile([P, width], F32, name="base%d" % n, tag="stage")
-            nc.sync.dma_start(out=part[:], in_=base[:, col : col + width])
-            base_parts.append(part)
-            col = col + width
+        grouped_dq = interleave(raw_dq, "grouped_dq")
 
         picked_kb = gather(key_bytes, U8, "picked_kb")
         picked_kw = gather(key_words, U16, "picked_kw")
         mx_q = quantize(grouped_q, "q")
         a = product(mx_q, picked_kw, picked_kb, "a")
-        mx_dq = quantize(grouped_dq, "dq")
-        ta = product(mx_dq, picked_kw, picked_kb, "ta")
         picked_vw = gather(val_words, U16, "picked_vw")
         mx_g = quantize(grouped_g, "g")
         picked_vb = gather(val_bytes, U8, "picked_vb")
         c = product(mx_g, picked_vw, picked_vb, "c")
+        mx_dq = quantize(grouped_dq, "dq")
+        ta = product(mx_dq, picked_kw, picked_kb, "ta")
 
-        e, th, th2, rs1 = wide("e"), wide("th"), wide("th2"), wide("rs1")
+        base_parts = []
+        col = 0
+        for n, width in enumerate(BASE_PARTS):
+            part = keep.tile([P, width], F32, name="base%d" % n, tag=("q_then_base", "words_then_base")[n])
+            nc.sync.dma_start(out=part[:], in_=base[:, col : col + width])
+            base_parts.append(part)
+            col = col + width
+
+        e = keep.tile([P, I], F32, name="e", tag="g_then_e")
+        th = keep.tile([P, I], F32, name="th", tag="dq_then_th")
+        th2 = wide("th2")
+        rs1 = [keep.tile([P, HALF], F32, name="rs1_%d" % half) for half in range(2)]
+        se_first = keep.tile([P, HALF], F32, name="se_first")
+        se_r4 = keep.tile([P, I], F32, name="se_r4", tag="turn")
         sum_e, sum_th = column("sum_e"), column("sum_th")
         nc.scalar.activation(e[:], a[:], ACT.Exp, accum_out=sum_e[:])
         nc.scalar.activation(th[:], a[:], ACT.Tanh, scale=0.5, accum_out=sum_th[:])
+        nc.scalar.activation(se_r4[:], e[:], ACT.Identity, bias=r4[:], scale=s[:])
         nc.scalar.activation(th2[:], th[:], ACT.Square)
-        nc.scalar.activation(rs1[:], th2[:], ACT.Identity, bias=r4[:], scale=nr4[:])
-
-        se_r4, se = wide("se_r4"), wide("se")
-        nc.gpsimd.tensor_scalar(se_r4[:], e[:], s[:], r4[:], ALU.mult, ALU.add)
-        nc.gpsimd.tensor_scalar(se[:], e[:], s[:], 0.0, ALU.mult, ALU.add)
-
-        z_sig, z, rz, nscale, nscale_rz = column("z_sig"), column("z"), column("rz"), column("nscale"), column("nscale_rz")
+        z_sig, z = column("z_sig"), column("z")
         nc.scalar.activation(z_sig[:], sum_th[:], ACT.Identity, bias=r2i[:], scale=r2[:])
+        nc.scalar.activation(se_first[:], e[:, 0:HALF], ACT.Copy, scale=s[:])
+        nc.scalar.activation(rs1[0][:], th2[:, 0:HALF], ACT.Identity, bias=r4[:], scale=nr4[:])
         nc.scalar.activation(z[:], sum_e[:], ACT.Identity, bias=z_sig[:], scale=s[:])
+        nc.scalar.activation(rs1[1][:], th2[:, HALF:I], ACT.Identity, bias=r4[:], scale=nr4[:])
 
-        p1 = wide("p1")
-        nc.vector.scalar_tensor_tensor(p1[:], th2[:], nr4[:], se_r4[:], ALU.mult, ALU.add)
-        nc.vector.reciprocal(rz[:], z[:])
-        nc.scalar.activation(nscale[:], rz[:], ACT.Copy, scale=-512.0)
-        nc.scalar.activation(nscale_rz[:], rz[:], ACT.Copy, scale=nscale[:])
+        p1_rz = keep.tile([P, I + 8], F32, name="p1_rz", tag="bytes_then_p1")
+        p1, rz = p1_rz[:, 0:I], p1_rz[:, I : I + 1]
+        nc.vector.scalar_tensor_tensor(p1, th2[:], nr4[:], se_r4[:], ALU.mult, ALU.add)
+        nc.vector.reciprocal(rz, z[:])
+        nscale, nscale_rz = column("nscale"), column("nscale_rz")
+        nc.scalar.activation(nscale[:], rz, ACT.Copy, scale=-512.0)
+        nc.scalar.activation(nscale_rz[:], rz, ACT.Copy, scale=nscale[:])
 
-        trs1, p2 = wide("trs1"), wide("p2")
-        nc.gpsimd.tensor_tensor(trs1[:], th[:], rs1[:], ALU.mult)
-        nc.gpsimd.tensor_tensor(p2[:], se[:], trs1[:], ALU.subtract)
+        trs1 = [keep.tile([P, HALF], F32, name="trs1_0", tag="turn"), keep.tile([P, HALF], F32, name="trs1_1")]
+        p2 = [keep.tile([P, HALF], F32, name="p2_%d" % half) for half in range(2)]
+        nc.gpsimd.tensor_tensor(trs1[0][:], th[:, 0:HALF], rs1[0][:], ALU.mult)
+        nc.gpsimd.tensor_tensor(p2[0][:], se_first[:], trs1[0][:], ALU.subtract)
 
         sum_ce, sum_ct, sum_cp, mean_c = column("sum_ce"), column("sum_ct"), column("sum_cp"), column("mean_c")
         ce, ct = wide("ce"), wide("ct")
         nc.vector.scalar_tensor_tensor(ce[:], c[:], s[:], e[:], ALU.mult, ALU.mult, accum_out=sum_ce[:])
         nc.vector.scalar_tensor_tensor(ct[:], th[:], 1.0, c[:], ALU.add, ALU.mult, accum_out=sum_ct[:])
         nc.scalar.activation(sum_cp[:], sum_ct[:], ACT.Identity, bias=sum_ce[:], scale=r2[:])
-        nc.scalar.activation(mean_c[:], sum_cp[:], ACT.Copy, scale=rz[:])
+        nc.scalar.activation(mean_c[:], sum_cp[:], ACT.Copy, scale=rz)
 
         tp, tz = wide("tp"), column("tz")
-        nc.vector.scalar_tensor_tensor(tp[:], ta[:], 1.0, p1[:], ALU.mult, ALU.mult, accum_out=tz[:])
+        nc.vector.scalar_tensor_tensor(tp[:], ta[:], 1.0, p1, ALU.mult, ALU.mult, accum_out=tz[:])
         p1n = wide("p1n")
-        nc.scalar.activation(p1n[:], p1[:], ACT.Copy, scale=nscale_rz[:])
+        nc.scalar.activation(p1n[:], p1, ACT.Copy, scale=nscale_rz[:])
 
         ctp, sum_ctp = wide("ctp"), column("sum_ctp")
         nc.vector.scalar_tensor_tensor(ctp[:], c[:], mean_c[:], tp[:], ALU.subtract, ALU.mult, accum_out=sum_ctp[:])
-        row_term = wide("row_term")
-        nc.scalar.activation(row_term[:], p1n[:], ACT.Copy, scale=sum_ctp[:])
 
-        t2n, slope, slot_term = wide("t2n"), wide("slope"), wide("slot_term")
-        nc.vector.scalar_tensor_tensor(t2n[:], ta[:], nscale[:], p2[:], ALU.mult, ALU.mult)
-        nc.vector.scalar_tensor_tensor(slope[:], p1n[:], tz[:], t2n[:], ALU.mult, ALU.subtract)
-        nc.vector.scalar_tensor_tensor(slot_term[:], c[:], mean_c[:], slope[:], ALU.subtract, ALU.mult)
-        nc.vector.tensor_tensor(window[:].indirect(offsets[:]), slot_term[:], row_term[:], ALU.add)
+        def slot_term(half):
+            cols = slice(half * HALF, (half + 1) * HALF)
+            t2n = keep.tile([P, HALF], F32, name="t2n%d" % half)
+            slope = keep.tile([P, HALF], F32, name="slope%d" % half)
+            term = keep.tile([P, HALF], F32, name="slot_term%d" % half)
+            nc.vector.scalar_tensor_tensor(t2n[:], ta[:, cols], nscale[:], p2[half][:], ALU.mult, ALU.mult)
+            nc.vector.scalar_tensor_tensor(slope[:], p1n[:, cols], tz[:], t2n[:], ALU.mult, ALU.subtract)
+            nc.vector.scalar_tensor_tensor(term[:], c[:, cols], mean_c[:], slope[:], ALU.subtract, ALU.mult)
+            return term
+
+        row_term = keep.tile([P, HALF], F32, name="row_term")
+        nc.scalar.activation(row_term[:], p1n[:, HALF:I], ACT.Copy, scale=sum_ctp[:])
+        first = slot_term(0)
+        gs_first = keep.tile([P, HALF], F32, name="gs_first")
+        nc.vector.scalar_tensor_tensor(gs_first[:], p1n[:, 0:HALF], sum_ctp[:], first[:], ALU.mult, ALU.add)
+        nc.scalar.activation(window[:].indirect(offsets[:, 0 : HALF // 16]), gs_first[:], ACT.Copy)
+        nc.vector.tensor_tensor(trs1[1][:], th[:, HALF:I], rs1[1][:], ALU.mult)
+        nc.vector.scalar_tensor_tensor(p2[1][:], e[:, HALF:I], s[:], trs1[1][:], ALU.mult, ALU.subtract)
+        second = slot_term(1)
+        nc.vector.tensor_tensor(window[:].indirect(offsets[:, HALF // 16 : I // 16]), second[:], row_term[:], ALU.add)
 
         col = 0
         for n, widths in enumerate(STORE_PARTS):

@@ -46,32 +46,33 @@ def tile_attend_hvmixedparts_s_kernel(tc, query, keys_words, keys_scales, share,
         nc.vector.memset(val_bytes[:].bitcast(I32), 0)
         nc.vector.memset(window[:], 0.0)
 
-        def load_bytes(queue, tile, src, quads):
-            for quad in quads:
-                queue.dma_start(out=tile[32 * quad : 32 * quad + 4, :].bitcast(I32), in_=src[0, 4 * quad : 4 * quad + 4, :].bitcast(I32))
+        def load_bytes(tile, src):
+            for quad in range(4):
+                nc.sync.dma_start(out=tile[32 * quad : 32 * quad + 4, :].bitcast(I32), in_=src[0, 4 * quad : 4 * quad + 4, :].bitcast(I32))
 
-        def load_rows(queue, tag, src, name):
+        def load_rows(tag, src, name):
             raw = keep.tile([P, PACK, Q], F32, name=name, tag=tag)
-            queue.dma_start(out=raw[:], in_=src.rearrange("(p j) w -> p j w", j=PACK))
+            nc.sync.dma_start(out=raw[:], in_=src.rearrange("(p j) w -> p j w", j=PACK))
             return raw
 
         s = column("s")
+        nc.gpsimd.dma_start(out=s[:], in_=share)
         nc.sync.dma_start(offsets[:], offs)
-        nc.scalar.dma_start(out=s[:], in_=share)
         nc.sync.dma_start(out=key_words[:].bitcast(I32), in_=keys_words[0].bitcast(I32))
-        load_bytes(nc.sync, key_bytes, keys_scales, (0, 1))
-        load_bytes(nc.scalar, key_bytes, keys_scales, (2, 3))
-        raw_q = load_rows(nc.scalar, "q_then_base", query, "raw_q")
-        raw_dq = load_rows(nc.gpsimd, "dq_then_th", dquery, "raw_dq")
-        raw_g = load_rows(nc.sync, "g_then_e", gout, "raw_g")
+        load_bytes(key_bytes, keys_scales)
+        raw_q = load_rows("q_then_base", query, "raw_q")
+        raw_dq = load_rows("dq_then_th", dquery, "raw_dq")
+        raw_g = load_rows("g_then_e", gout, "raw_g")
         nc.sync.dma_start(out=val_words[:].bitcast(I32), in_=vals_words[0].bitcast(I32))
-        load_bytes(nc.sync, val_bytes, vals_scales, range(4))
+        load_bytes(val_bytes, vals_scales)
 
-        r4, nr4, r2, r2i = column("r4"), column("nr4"), column("r2"), column("r2i")
+        r4, nr4, r2, nr2, r2i, ns = column("r4"), column("nr4"), column("r2"), column("nr2"), column("r2i"), column("ns")
         nc.gpsimd.tensor_scalar(r4[:], s[:], -0.75, 0.75, ALU.mult, ALU.add)
         nc.gpsimd.tensor_scalar(nr4[:], s[:], 0.75, -0.75, ALU.mult, ALU.add)
         nc.gpsimd.tensor_scalar(r2[:], s[:], -1.5, 1.5, ALU.mult, ALU.add)
+        nc.gpsimd.tensor_scalar(nr2[:], s[:], 1.5, -1.5, ALU.mult, ALU.add)
         nc.gpsimd.tensor_scalar(r2i[:], s[:], -1.5 * I, 1.5 * I, ALU.mult, ALU.add)
+        nc.gpsimd.tensor_scalar(ns[:], s[:], -1.0, 1.0, ALU.mult, ALU.mult)
 
         def interleave(raw, name):
             grouped = keep.tile([P, Q, PACK], BF16, name=name, align_bytes=64)
@@ -95,19 +96,19 @@ def tile_attend_hvmixedparts_s_kernel(tc, query, keys_words, keys_scales, share,
             return acc
 
         grouped_q = interleave(raw_q, "grouped_q")
-        grouped_g = interleave(raw_g, "grouped_g")
         grouped_dq = interleave(raw_dq, "grouped_dq")
+        grouped_g = interleave(raw_g, "grouped_g")
 
         picked_kb = gather(key_bytes, U8, "picked_kb")
         picked_kw = gather(key_words, U16, "picked_kw")
         mx_q = quantize(grouped_q, "q")
         a = product(mx_q, picked_kw, picked_kb, "a")
+        mx_dq = quantize(grouped_dq, "dq")
+        ta = product(mx_dq, picked_kw, picked_kb, "ta")
         picked_vw = gather(val_words, U16, "picked_vw")
         mx_g = quantize(grouped_g, "g")
         picked_vb = gather(val_bytes, U8, "picked_vb")
         c = product(mx_g, picked_vw, picked_vb, "c")
-        mx_dq = quantize(grouped_dq, "dq")
-        ta = product(mx_dq, picked_kw, picked_kb, "ta")
 
         base_parts = []
         col = 0
@@ -119,70 +120,58 @@ def tile_attend_hvmixedparts_s_kernel(tc, query, keys_words, keys_scales, share,
 
         e = keep.tile([P, I], F32, name="e", tag="g_then_e")
         th = keep.tile([P, I], F32, name="th", tag="dq_then_th")
-        th2 = wide("th2")
-        rs1 = [keep.tile([P, HALF], F32, name="rs1_%d" % half) for half in range(2)]
-        se_first = keep.tile([P, HALF], F32, name="se_first")
-        se_r4 = keep.tile([P, I], F32, name="se_r4", tag="turn")
-        sum_e, sum_th = column("sum_e"), column("sum_th")
+        th2 = keep.tile([P, I], F32, name="th2", tag="th2_then_c_terms")
+        rs1, se = wide("rs1"), wide("se")
+        se_r4 = wide("se_r4")
+        sum_e, sum_th, z_sig, z = column("sum_e"), column("sum_th"), column("z_sig"), column("z")
         nc.scalar.activation(e[:], a[:], ACT.Exp, accum_out=sum_e[:])
         nc.scalar.activation(th[:], a[:], ACT.Tanh, scale=0.5, accum_out=sum_th[:])
-        nc.scalar.activation(se_r4[:], e[:], ACT.Identity, bias=r4[:], scale=s[:])
         nc.scalar.activation(th2[:], th[:], ACT.Square)
-        z_sig, z = column("z_sig"), column("z")
+        nc.scalar.activation(rs1[:], th2[:], ACT.Identity, bias=r4[:], scale=nr4[:])
         nc.scalar.activation(z_sig[:], sum_th[:], ACT.Identity, bias=r2i[:], scale=r2[:])
-        nc.scalar.activation(se_first[:], e[:, 0:HALF], ACT.Copy, scale=s[:])
-        nc.scalar.activation(rs1[0][:], th2[:, 0:HALF], ACT.Identity, bias=r4[:], scale=nr4[:])
         nc.scalar.activation(z[:], sum_e[:], ACT.Identity, bias=z_sig[:], scale=s[:])
-        nc.scalar.activation(rs1[1][:], th2[:, HALF:I], ACT.Identity, bias=r4[:], scale=nr4[:])
+        nc.gpsimd.tensor_scalar(se_r4[:], e[:], s[:], r4[:], ALU.mult, ALU.add)
+        nc.gpsimd.tensor_scalar(se[:], e[:], s[:], 0.0, ALU.mult, ALU.add)
 
         p1_rz = keep.tile([P, I + 8], F32, name="p1_rz", tag="bytes_then_p1")
         p1, rz = p1_rz[:, 0:I], p1_rz[:, I : I + 1]
         nc.vector.scalar_tensor_tensor(p1, th2[:], nr4[:], se_r4[:], ALU.mult, ALU.add)
-        nc.vector.reciprocal(rz, z[:])
-        nscale, nscale_rz = column("nscale"), column("nscale_rz")
-        nc.scalar.activation(nscale[:], rz, ACT.Copy, scale=-512.0)
-        nc.scalar.activation(nscale_rz[:], rz, ACT.Copy, scale=nscale[:])
 
-        trs1 = [keep.tile([P, HALF], F32, name="trs1_0", tag="turn"), keep.tile([P, HALF], F32, name="trs1_1")]
+        trs1 = wide("trs1")
         p2 = [keep.tile([P, HALF], F32, name="p2_%d" % half) for half in range(2)]
-        nc.gpsimd.tensor_tensor(trs1[0][:], th[:, 0:HALF], rs1[0][:], ALU.mult)
-        nc.gpsimd.tensor_tensor(p2[0][:], se_first[:], trs1[0][:], ALU.subtract)
+        nc.gpsimd.tensor_tensor(trs1[:], th[:], rs1[:], ALU.mult)
+        nc.gpsimd.tensor_tensor(p2[0][:], se[:, 0:HALF], trs1[:, 0:HALF], ALU.subtract)
+        nc.gpsimd.tensor_tensor(p2[1][:], se[:, HALF:I], trs1[:, HALF:I], ALU.subtract)
 
-        sum_ce, sum_ct, sum_cp, mean_c = column("sum_ce"), column("sum_ct"), column("sum_cp"), column("mean_c")
-        ce, ct = wide("ce"), wide("ct")
-        nc.vector.scalar_tensor_tensor(ce[:], c[:], s[:], e[:], ALU.mult, ALU.mult, accum_out=sum_ce[:])
-        nc.vector.scalar_tensor_tensor(ct[:], th[:], 1.0, c[:], ALU.add, ALU.mult, accum_out=sum_ct[:])
-        nc.scalar.activation(sum_cp[:], sum_ct[:], ACT.Identity, bias=sum_ce[:], scale=r2[:])
-        nc.scalar.activation(mean_c[:], sum_cp[:], ACT.Copy, scale=rz)
+        ntp, ntz = wide("ntp"), column("ntz")
+        nc.vector.scalar_tensor_tensor(ntp[:], ta[:], -1.0, p1, ALU.mult, ALU.mult, accum_out=ntz[:])
+        nc.vector.reciprocal(rz, z[:])
+        scale, scale_rz, p1s = column("scale"), column("scale_rz"), wide("p1s")
+        nc.scalar.activation(scale[:], rz, ACT.Copy, scale=512.0)
+        nc.scalar.activation(scale_rz[:], rz, ACT.Copy, scale=scale[:])
+        nc.scalar.activation(p1s[:], p1, ACT.Copy, scale=scale_rz[:])
 
-        tp, tz = wide("tp"), column("tz")
-        nc.vector.scalar_tensor_tensor(tp[:], ta[:], 1.0, p1, ALU.mult, ALU.mult, accum_out=tz[:])
-        p1n = wide("p1n")
-        nc.scalar.activation(p1n[:], p1, ACT.Copy, scale=nscale_rz[:])
+        c_terms = keep.tile([P, 2, I], F32, name="c_terms", tag="th2_then_c_terms")
+        sum_nce, sum_ct, sum_ncp, nmean = column("sum_nce"), column("sum_ct"), column("sum_ncp"), column("nmean")
+        nc.vector.scalar_tensor_tensor(c_terms[:, 0, :], c[:], ns[:], e[:], ALU.mult, ALU.mult, accum_out=sum_nce[:])
+        nc.vector.scalar_tensor_tensor(c_terms[:, 1, :], th[:], 1.0, c[:], ALU.add, ALU.mult, accum_out=sum_ct[:])
+        nc.scalar.activation(sum_ncp[:], sum_ct[:], ACT.Identity, bias=sum_nce[:], scale=nr2[:])
+        nc.scalar.activation(nmean[:], sum_ncp[:], ACT.Copy, scale=rz)
 
-        ctp, sum_ctp = wide("ctp"), column("sum_ctp")
-        nc.vector.scalar_tensor_tensor(ctp[:], c[:], mean_c[:], tp[:], ALU.subtract, ALU.mult, accum_out=sum_ctp[:])
+        nctp, sum_nctp, row_factor, row_term = wide("nctp"), column("sum_nctp"), column("row_factor"), wide("row_term")
+        nc.vector.scalar_tensor_tensor(nctp[:], c[:], 1.0, ntp[:], ALU.mult, ALU.mult, accum_out=sum_nctp[:])
+        nc.scalar.activation(row_factor[:], nmean[:], ACT.Identity, bias=sum_nctp[:], scale=ntz[:])
+        nc.scalar.activation(row_term[:], p1s[:], ACT.Copy, scale=row_factor[:])
 
-        def slot_term(half):
-            cols = slice(half * HALF, (half + 1) * HALF)
-            t2n = keep.tile([P, HALF], F32, name="t2n%d" % half)
-            slope = keep.tile([P, HALF], F32, name="slope%d" % half)
-            term = keep.tile([P, HALF], F32, name="slot_term%d" % half)
-            nc.vector.scalar_tensor_tensor(t2n[:], ta[:, cols], nscale[:], p2[half][:], ALU.mult, ALU.mult)
-            nc.vector.scalar_tensor_tensor(slope[:], p1n[:, cols], tz[:], t2n[:], ALU.mult, ALU.subtract)
-            nc.vector.scalar_tensor_tensor(term[:], c[:, cols], mean_c[:], slope[:], ALU.subtract, ALU.mult)
-            return term
-
-        row_term = keep.tile([P, HALF], F32, name="row_term")
-        nc.scalar.activation(row_term[:], p1n[:, HALF:I], ACT.Copy, scale=sum_ctp[:])
-        first = slot_term(0)
-        gs_first = keep.tile([P, HALF], F32, name="gs_first")
-        nc.vector.scalar_tensor_tensor(gs_first[:], p1n[:, 0:HALF], sum_ctp[:], first[:], ALU.mult, ALU.add)
-        nc.scalar.activation(window[:].indirect(offsets[:, 0 : HALF // 16]), gs_first[:], ACT.Copy)
-        nc.vector.tensor_tensor(trs1[1][:], th[:, HALF:I], rs1[1][:], ALU.mult)
-        nc.vector.scalar_tensor_tensor(p2[1][:], e[:, HALF:I], s[:], trs1[1][:], ALU.mult, ALU.subtract)
-        second = slot_term(1)
-        nc.vector.tensor_tensor(window[:].indirect(offsets[:, HALF // 16 : I // 16]), second[:], row_term[:], ALU.add)
+        halves = [slice(half * HALF, (half + 1) * HALF) for half in range(2)]
+        t2, slope, slot_term = wide("t2"), wide("slope"), wide("slot_term")
+        for half, cols in enumerate(halves):
+            nc.vector.scalar_tensor_tensor(t2[:, cols], ta[:, cols], scale[:], p2[half][:], ALU.mult, ALU.mult)
+        for cols in halves:
+            nc.vector.scalar_tensor_tensor(slope[:, cols], p1s[:, cols], ntz[:], t2[:, cols], ALU.mult, ALU.add)
+        for cols in halves:
+            nc.vector.scalar_tensor_tensor(slot_term[:, cols], c[:, cols], nmean[:], slope[:, cols], ALU.add, ALU.mult)
+        nc.vector.tensor_tensor(window[:].indirect(offsets[:]), slot_term[:], row_term[:], ALU.add)
 
         col = 0
         for n, widths in enumerate(STORE_PARTS):

from contextlib import ExitStack

import concourse.mybir as mybir

D, T, I, Q = 512, 2048, 512, 128
FLOPS = 3 * 2 * D * Q * I

F32 = mybir.dt.float32
BF16 = mybir.dt.bfloat16
I32 = mybir.dt.int32
U32 = mybir.dt.uint32
U16 = mybir.dt.uint16
U8 = mybir.dt.uint8
FP8X4 = mybir.dt.float8_e4m3fn_x4
FP4X4 = mybir.dt.float4_e2m1fn_x4
ALU = mybir.AluOpType
ACT = mybir.ActivationFunctionType

P = 128
PACK = 4
BASE_PARTS = (1024, 1024)
STORE_PARTS = ((256, 384, 384), (512, 384, 128))
HALF = I // 2


def tile_attend_hvmixedparts_s_kernel(tc, query, keys_words, keys_scales, share, gout, vals_words, vals_scales, dquery, base, offs, out):
    nc = tc.nc
    with ExitStack() as ctx:
        keep = ctx.enter_context(tc.tile_pool(name="keep", bufs=1))
        psum = ctx.enter_context(tc.psum_pool(name="psum", bufs=1))

        def wide(name):
            return keep.tile([P, I], F32, name=name)

        def column(name):
            return keep.tile([P, 1], F32, name=name)

        offsets = keep.tile([P, I // 16], U16, name="offsets")
        key_words = keep.tile([P, T], U16, name="key_words", tag="words_then_base")
        key_bytes = keep.tile([P, T], U8, name="key_bytes")
        val_words = keep.tile([P, T], U16, name="val_words")
        val_bytes = keep.tile([P, T], U8, name="val_bytes", tag="bytes_then_p1")
        window = keep.tile([P, T], F32, name="window")

        nc.vector.memset(key_bytes[:].bitcast(I32), 0)
        nc.vector.memset(val_bytes[:].bitcast(I32), 0)
        nc.vector.memset(window[:], 0.0)

        def load_bytes(tile, src):
            for quad in range(4):
                nc.sync.dma_start(out=tile[32 * quad : 32 * quad + 4, :].bitcast(I32), in_=src[0, 4 * quad : 4 * quad + 4, :].bitcast(I32))

        def load_rows(tag, src, name):
            raw = keep.tile([P, PACK, Q], F32, name=name, tag=tag)
            nc.sync.dma_start(out=raw[:], in_=src.rearrange("(p j) w -> p j w", j=PACK))
            return raw

        s = column("s")
        nc.gpsimd.dma_start(out=s[:], in_=share)
        nc.sync.dma_start(offsets[:], offs)
        nc.sync.dma_start(out=key_words[:].bitcast(I32), in_=keys_words[0].bitcast(I32))
        load_bytes(key_bytes, keys_scales)
        raw_q = load_rows("q_then_base", query, "raw_q")
        raw_dq = load_rows("dq_then_th", dquery, "raw_dq")
        raw_g = load_rows("g_then_e", gout, "raw_g")
        nc.sync.dma_start(out=val_words[:].bitcast(I32), in_=vals_words[0].bitcast(I32))
        load_bytes(val_bytes, vals_scales)

        r4, nr4, r2, nr2, r2i, ns = column("r4"), column("nr4"), column("r2"), column("nr2"), column("r2i"), column("ns")
        nc.gpsimd.tensor_scalar(r4[:], s[:], -0.75, 0.75, ALU.mult, ALU.add)
        nc.gpsimd.tensor_scalar(nr4[:], s[:], 0.75, -0.75, ALU.mult, ALU.add)
        nc.gpsimd.tensor_scalar(r2[:], s[:], -1.5, 1.5, ALU.mult, ALU.add)
        nc.gpsimd.tensor_scalar(nr2[:], s[:], 1.5, -1.5, ALU.mult, ALU.add)
        nc.gpsimd.tensor_scalar(r2i[:], s[:], -1.5 * I, 1.5 * I, ALU.mult, ALU.add)
        nc.gpsimd.tensor_scalar(ns[:], s[:], -1.0, 1.0, ALU.mult, ALU.mult)

        def interleave(raw, name):
            grouped = keep.tile([P, Q, PACK], BF16, name=name, align_bytes=64)
            nc.scalar.activation(grouped[:], raw[:].rearrange("p j w -> p w j"), ACT.Copy)
            return grouped

        def quantize(grouped, name):
            codes = keep.tile([P, Q], U32, name=name + "_codes", align_bytes=64)
            scales = keep.tile([P, Q], U8, name=name + "_scales", align_bytes=64)
            nc.vector.quantize_mx(out=codes[:].bitcast(FP8X4), scales=scales[:], in_=grouped[:].rearrange("p w j -> p (w j)"))
            return codes, scales

        def gather(tile, dtype, name):
            picked = keep.tile([P, I], dtype, name=name, align_bytes=64)
            nc.vector.tensor_copy(picked[:], tile[:].indirect(offsets[:]))
            return picked

        def product(rows, words, scale_bytes, name):
            acc = psum.tile([P, I], F32, name=name)
            nc.tensor.matmul_mx(out=acc[:], lhsT=rows[0][:].bitcast(FP8X4), lhsT_scale=rows[1][:], rhs=words[:].bitcast(FP4X4), rhs_scale=scale_bytes[:], start=True, stop=True)
            return acc

        grouped_q = interleave(raw_q, "grouped_q")
        grouped_dq = interleave(raw_dq, "grouped_dq")
        grouped_g = interleave(raw_g, "grouped_g")

        picked_kb = gather(key_bytes, U8, "picked_kb")
        picked_kw = gather(key_words, U16, "picked_kw")
        mx_q = quantize(grouped_q, "q")
        a = product(mx_q, picked_kw, picked_kb, "a")
        mx_dq = quantize(grouped_dq, "dq")
        ta = product(mx_dq, picked_kw, picked_kb, "ta")
        picked_vw = gather(val_words, U16, "picked_vw")
        mx_g = quantize(grouped_g, "g")
        picked_vb = gather(val_bytes, U8, "picked_vb")
        c = product(mx_g, picked_vw, picked_vb, "c")

        base_parts = []
        col = 0
        for n, width in enumerate(BASE_PARTS):
            part = keep.tile([P, width], F32, name="base%d" % n, tag=("q_then_base", "words_then_base")[n])
            nc.sync.dma_start(out=part[:], in_=base[:, col : col + width])
            base_parts.append(part)
            col = col + width

        e = keep.tile([P, I], F32, name="e", tag="g_then_e")
        th = keep.tile([P, I], F32, name="th", tag="dq_then_th")
        th2 = keep.tile([P, I], F32, name="th2", tag="th2_then_c_terms")
        rs1, se = wide("rs1"), wide("se")
        se_r4 = wide("se_r4")
        sum_e, sum_th, z_sig, z = column("sum_e"), column("sum_th"), column("z_sig"), column("z")
        nc.scalar.activation(e[:], a[:], ACT.Exp, accum_out=sum_e[:])
        nc.scalar.activation(th[:], a[:], ACT.Tanh, scale=0.5, accum_out=sum_th[:])
        nc.scalar.activation(th2[:], th[:], ACT.Square)
        nc.scalar.activation(rs1[:], th2[:], ACT.Identity, bias=r4[:], scale=nr4[:])
        nc.scalar.activation(z_sig[:], sum_th[:], ACT.Identity, bias=r2i[:], scale=r2[:])
        nc.scalar.activation(z[:], sum_e[:], ACT.Identity, bias=z_sig[:], scale=s[:])
        nc.gpsimd.tensor_scalar(se_r4[:], e[:], s[:], r4[:], ALU.mult, ALU.add)
        nc.gpsimd.tensor_scalar(se[:], e[:], s[:], 0.0, ALU.mult, ALU.add)

        p1_rz = keep.tile([P, I + 8], F32, name="p1_rz", tag="bytes_then_p1")
        p1, rz = p1_rz[:, 0:I], p1_rz[:, I : I + 1]
        nc.vector.scalar_tensor_tensor(p1, th2[:], nr4[:], se_r4[:], ALU.mult, ALU.add)

        trs1 = wide("trs1")
        p2 = [keep.tile([P, HALF], F32, name="p2_%d" % half) for half in range(2)]
        nc.gpsimd.tensor_tensor(trs1[:], th[:], rs1[:], ALU.mult)
        nc.gpsimd.tensor_tensor(p2[0][:], se[:, 0:HALF], trs1[:, 0:HALF], ALU.subtract)
        nc.gpsimd.tensor_tensor(p2[1][:], se[:, HALF:I], trs1[:, HALF:I], ALU.subtract)

        ntp, ntz = wide("ntp"), column("ntz")
        nc.vector.scalar_tensor_tensor(ntp[:], ta[:], -1.0, p1, ALU.mult, ALU.mult, accum_out=ntz[:])
        nc.vector.reciprocal(rz, z[:])
        scale, scale_rz, p1s = column("scale"), column("scale_rz"), wide("p1s")
        nc.scalar.activation(scale[:], rz, ACT.Copy, scale=512.0)
        nc.scalar.activation(scale_rz[:], rz, ACT.Copy, scale=scale[:])
        nc.scalar.activation(p1s[:], p1, ACT.Copy, scale=scale_rz[:])

        c_terms = keep.tile([P, 2, I], F32, name="c_terms", tag="th2_then_c_terms")
        sum_nce, sum_ct, sum_ncp, nmean = column("sum_nce"), column("sum_ct"), column("sum_ncp"), column("nmean")
        nc.vector.scalar_tensor_tensor(c_terms[:, 0, :], c[:], ns[:], e[:], ALU.mult, ALU.mult, accum_out=sum_nce[:])
        nc.vector.scalar_tensor_tensor(c_terms[:, 1, :], th[:], 1.0, c[:], ALU.add, ALU.mult, accum_out=sum_ct[:])
        nc.scalar.activation(sum_ncp[:], sum_ct[:], ACT.Identity, bias=sum_nce[:], scale=nr2[:])
        nc.scalar.activation(nmean[:], sum_ncp[:], ACT.Copy, scale=rz)

        nctp, sum_nctp, row_factor, row_term = wide("nctp"), column("sum_nctp"), column("row_factor"), wide("row_term")
        nc.vector.scalar_tensor_tensor(nctp[:], c[:], 1.0, ntp[:], ALU.mult, ALU.mult, accum_out=sum_nctp[:])
        nc.scalar.activation(row_factor[:], nmean[:], ACT.Identity, bias=sum_nctp[:], scale=ntz[:])
        nc.scalar.activation(row_term[:], p1s[:], ACT.Copy, scale=row_factor[:])

        halves = [slice(half * HALF, (half + 1) * HALF) for half in range(2)]
        t2, slope, slot_term = wide("t2"), wide("slope"), wide("slot_term")
        for half, cols in enumerate(halves):
            nc.vector.scalar_tensor_tensor(t2[:, cols], ta[:, cols], scale[:], p2[half][:], ALU.mult, ALU.mult)
        for cols in halves:
            nc.vector.scalar_tensor_tensor(slope[:, cols], p1s[:, cols], ntz[:], t2[:, cols], ALU.mult, ALU.add)
        for cols in halves:
            nc.vector.scalar_tensor_tensor(slot_term[:, cols], c[:, cols], nmean[:], slope[:, cols], ALU.add, ALU.mult)
        nc.vector.tensor_tensor(window[:].indirect(offsets[:]), slot_term[:], row_term[:], ALU.add)

        col = 0
        for n, widths in enumerate(STORE_PARTS):
            inner = 0
            for m, width in enumerate(widths):
                result = keep.tile([P, width], F32, name="result%d_%d" % (n, m))
                nc.vector.tensor_tensor(result[:], window[:, col : col + width], base_parts[n][:, inner : inner + width], ALU.add)
                nc.sync.dma_start(out=out[:, col : col + width], in_=result[:])
                col = col + width
                inner = inner + width
